import numpy as np
import ml_dtypes


def mxq(x, axis, fmt="e4m3"):
    dtype, down = {"e4m3": (ml_dtypes.float8_e4m3fn, 7), "e5m2": (ml_dtypes.float8_e5m2, 14)}[fmt]
    v = np.moveaxis(np.asarray(x, np.float32).astype(ml_dtypes.bfloat16).astype(np.float64), axis, -1)
    blocks = v.reshape(v.shape[:-1] + (-1, 32))
    amax = np.abs(blocks).max(-1, keepdims=True)
    byte = np.maximum(np.where(amax > 0, np.frexp(amax)[1] - 1 + 127, 0) - down, 1)
    scale = np.exp2(byte - 127.0)
    codes = (blocks / scale).astype(np.float32).astype(dtype).astype(np.float64)
    return np.moveaxis((codes * scale).reshape(v.shape), -1, axis)


WIDE = False


def mx_kscale(k):
    if not WIDE:
        return np.ones(k)
    levels = np.array([30, -30])
    if k % 512:
        return np.exp2(np.random.permutation(np.resize(levels, k // 32))).repeat(32)
    a = np.empty((k // 512, 16))
    for p in range(k // 512):
        a[p, :8] = np.random.permutation(np.resize(levels, 8))
        for g in range(8):
            far = levels[np.abs(levels - a[p, g]) >= 10]
            a[p, g + 8] = far[np.random.randint(len(far))]
    return np.exp2(a.ravel()).repeat(32)


def f64(x):
    return np.asarray(x).astype(np.float64)


def striped(idx):
    return np.tile(np.asarray(idx).reshape(-1, 16).T, (8, 1)).astype(np.uint16)


def unstriped(offs):
    return offs[:16].T.reshape(-1).astype(np.int64)


E2M1 = np.array([0.0, 0.5, 1.0, 1.5, 2.0, 3.0, 4.0, 6.0, -0.0, -0.5, -1.0, -1.5, -2.0, -3.0, -4.0, -6.0])


def pack_weight(w, fmt):
    k, n = w.shape
    w = f64(np.asarray(w, np.float32).astype(ml_dtypes.bfloat16)).reshape(k // 32, 32, n)
    amax = np.abs(w).max(1)
    if fmt == "e4m3":
        byte = np.frexp(amax)[1] - 1 + 127 - 7
    else:
        mant, ex = np.frexp(amax / 6.0)
        byte = np.where(mant > 0.5, ex, ex - 1) + 127
    byte = np.clip(np.where(amax > 0, byte, 1), 1, 254)
    scaled = (w * np.exp2(127.0 - byte)[:, None, :]).reshape(k, n).astype(np.float32)
    by_word = np.ascontiguousarray(scaled.reshape(k // 512, 128, 4, n).transpose(0, 1, 3, 2))
    if fmt == "e4m3":
        words = by_word.astype(ml_dtypes.float8_e4m3fn).view(np.uint8)
    else:
        c = by_word.astype(ml_dtypes.float4_e2m1fn).view(np.uint8) & 0xF
        words = (c[..., 0::2] | (c[..., 1::2] << 4)).reshape(k // 512, 128, 2 * n)
    return np.ascontiguousarray(words), np.ascontiguousarray(byte.astype(np.uint8).reshape(k // 512, 16, n))


def unpack_weight(words, scales, fmt):
    g, _, n = scales.shape
    words = np.ascontiguousarray(words).reshape(g, 128, n, -1)
    if fmt == "e4m3":
        vals = words.view(ml_dtypes.float8_e4m3fn).astype(np.float64)
    else:
        nib = np.empty((g, 128, n, 4), np.uint8)
        nib[..., 0::2] = words & 0xF
        nib[..., 1::2] = words >> 4
        vals = E2M1[nib]
    vals = vals * np.repeat(np.exp2(scales.astype(np.float64) - 127.0), 8, axis=1)[..., None]
    return vals.transpose(0, 1, 3, 2).reshape(g * 512, n)


K, T, J, R, F, Z, N, U = 512, 1024, 256, 512, 512, 1024, 256, 128


def setup_inputs():
    n = np.random.standard_normal
    idx = np.random.permutation(T)[:J]
    idx2 = np.random.permutation(Z)[:J]
    idx3 = np.random.permutation(J)[:U]
    idx4 = np.random.permutation(J)[:U]
    fk = mx_kscale(K)
    fr = mx_kscale(R)
    ff = mx_kscale(F)
    wp = pack_weight(n((K, R)) * 1 / np.sqrt(K) / fk[:, None] * fr, "e4m3")
    xop = pack_weight(n((F, Z)) / ff[:, None], "e4m3")
    w2p = pack_weight(n((F, R)) * 1 / np.sqrt(F) * ff[:, None] * fr, "e2m1")
    wbp = pack_weight(n((R, N)) * 1 / np.sqrt(R) / fr[:, None], "e2m1")
    return {
        "cq": (np.random.randint(-7, 8, (K, T)).astype(np.float64)).astype(np.float32),
        "ga": (np.random.uniform(0.1, 0.4, (K, 1)) * fk[:, None]).astype(np.float32),
        "w_words": wp[0],
        "w_scales": wp[1],
        "xo_words": xop[0],
        "xo_scales": xop[1],
        "w2_words": w2p[0],
        "w2_scales": w2p[1],
        "wb_words": wbp[0],
        "wb_scales": wbp[1],
        "so": (np.random.uniform(0.5, 1.6, (N, 1))).astype(np.float32),
        "offs": striped(idx),
        "offs2": striped(idx2),
        "offs3": striped(idx3),
        "offs4": striped(idx4),
    }


def reference(cq, ga, w_words, w_scales, xo_words, xo_scales, w2_words, w2_scales, wb_words, wb_scales, so, offs, offs2, offs3, offs4):
    idx = unstriped(offs)
    idx2 = unstriped(offs2)
    idx3 = unstriped(offs3)
    idx4 = unstriped(offs4)
    wu = unpack_weight(w_words, w_scales, "e4m3")
    xou = unpack_weight(xo_words, xo_scales, "e4m3")
    w2u = unpack_weight(w2_words, w2_scales, "e2m1")
    wbu = unpack_weight(wb_words, wb_scales, "e2m1")
    x1 = f64(cq)[:, idx] * f64(ga)
    x1q = mxq(x1, 0, "e4m3")
    a = wu.T @ x1q
    xoidx2g = xou[:, idx2]
    b = w2u.T @ xoidx2g
    hid = np.maximum(a, b)
    hidq = mxq(hid, 0, "e5m2")
    p = wbu.T @ hidq
    y = p[:, idx3] - p[:, idx4] * f64(so)
    return y

@@ -1,0 +1,191 @@
+from contextlib import ExitStack
+
+import concourse.mybir as mybir
+
+K, T, J, R, F, Z, N, U = 512, 1024, 256, 512, 512, 1024, 256, 128
+FLOPS = 2 * K * R * J + 2 * F * R * J + 2 * R * N * J
+
+F32 = mybir.dt.float32
+BF16 = mybir.dt.bfloat16
+I32 = mybir.dt.int32
+U32 = mybir.dt.uint32
+U16 = mybir.dt.uint16
+U8 = mybir.dt.uint8
+E4M3 = mybir.dt.float8_e4m3fn_x4
+E5M2 = mybir.dt.float8_e5m2_x4
+E2M1 = mybir.dt.float4_e2m1fn_x4
+COPY = mybir.ActivationFunctionType.Copy
+MAX = mybir.AluOpType.max
+SUB = mybir.AluOpType.subtract
+
+P = 128
+PACK = 4
+QUADS = 4
+HALF = J // 2
+
+
+def tile_list_meetdirect_codednote_one_weighedout_kernel(
+    tc, cq, ga, w_words, w_scales, xo_words, xo_scales, w2_words, w2_scales, wb_words, wb_scales, so,
+    offs, offs2, offs3, offs4, out,
+):
+    nc = tc.nc
+    with ExitStack() as ctx:
+        sb = ctx.enter_context(tc.tile_pool(name="sb", bufs=1))
+        ps = ctx.enter_context(tc.psum_pool(name="ps", bufs=1))
+
+        def tile(name, shape, dtype):
+            return sb.tile(shape, dtype, name=name, align_bytes=64)
+
+        l1 = tile("l1", [P, J // 16], U16)
+        l2 = tile("l2", [P, J // 16], U16)
+        l3 = tile("l3", [P, U // 16], U16)
+        l4 = tile("l4", [P, U // 16], U16)
+        ga_sb = tile("ga_sb", [P, PACK], F32)
+        so_sb = tile("so_sb", [P, 2], F32)
+        cq_sb = [tile("cq%d" % t, [P, T], F32) for t in range(PACK)]
+        xo_w = tile("xo_w", [P, Z], I32)
+        w_w = tile("w_w", [P, R], I32)
+        w2_w = tile("w2_w", [P, R // 2], I32)
+        wb_w = tile("wb_w", [P, 2 * N], U8)
+        xs_stage = tile("xs_stage", [PACK, QUADS, Z // 4], I32)
+        WS = (R + R + N) // 4
+        ws_stage = tile("ws_stage", [PACK, QUADS, WS], I32)
+        xs = tile("xs", [P, Z], U8)
+        ws = tile("ws", [P, R + R + N], U8)
+
+        def rows(scales):
+            return scales[0].bitcast(I32).rearrange("(q r) n -> r q n", r=PACK)
+
+        cq_rows = cq.rearrange("(p t) c -> p t c", t=PACK)
+
+        nc.sync.dma_start(l1[:], offs)
+        nc.scalar.dma_start(ga_sb[:], ga.rearrange("(p t) o -> p (t o)", t=PACK))
+        nc.sync.dma_start(l2[:], offs2)
+        nc.scalar.dma_start(xs_stage[:], rows(xo_scales))
+        nc.sync.dma_start(xo_w[:], xo_words[0].rearrange("p n t -> p (n t)").bitcast(I32))
+        nc.scalar.dma_start(ws_stage[:, :, R // 4 : R // 2], rows(w2_scales))
+        nc.sync.dma_start(cq_sb[0][:], cq_rows[:, 0, :])
+        nc.scalar.dma_start(ws_stage[:, :, 0 : R // 4], rows(w_scales))
+        nc.gpsimd.dma_start(ws_stage[:, :, R // 2 : WS], rows(wb_scales))
+        with nc.allow_non_contiguous_dma(reason="one value a partition"):
+            nc.gpsimd.dma_start(so_sb[:], so.rearrange("(m p) o -> p (m o)", p=P))
+        nc.sync.dma_start(w2_w[:], w2_words[0].bitcast(I32))
+        for t in range(1, PACK):
+            nc.sync.dma_start(cq_sb[t][:], cq_rows[:, t, :])
+        nc.sync.dma_start(w_w[:], w_words[0].rearrange("p n t -> p (n t)").bitcast(I32))
+        nc.sync.dma_start(wb_w[:].bitcast(I32), wb_words[0].bitcast(I32))
+        nc.sync.dma_start(l3[:], offs3)
+        nc.sync.dma_start(l4[:], offs4)
+
+        nc.vector.memset(xs[:].bitcast(I32), 0)
+        nc.vector.memset(ws[:].bitcast(I32), 0)
+        for q in range(QUADS):
+            nc.vector.tensor_copy(xs[32 * q : 32 * q + PACK, :].bitcast(I32), xs_stage[:, q, :])
+        xg_s = tile("xg_s", [P, J], U8)
+        nc.vector.tensor_copy(xg_s[:], xs[:].indirect(l2[:]))
+        xg_w = tile("xg_w", [P, J], U32)
+        nc.vector.tensor_copy(xg_w[:], xo_w[:].bitcast(U32).indirect(l2[:]))
+        for q in range(QUADS):
+            nc.vector.tensor_copy(ws[32 * q : 32 * q + PACK, :].bitcast(I32), ws_stage[:, q, :])
+        wp_s = tile("wp_s", [P, 2 * R], U8)
+        nc.vector.tensor_copy(
+            wp_s[:].rearrange("p (g t m) -> p g t m", g=2, t=PACK),
+            ws[:, 0 : 2 * R].rearrange("p (g m t) -> p g t m", g=2, t=PACK),
+        )
+        w2p = tile("w2p", [P, 2 * R], U8)
+        nc.vector.tensor_copy(
+            w2p[:].bitcast(U16).rearrange("p (t m) -> p t m", t=PACK),
+            w2_w[:].bitcast(U16).rearrange("p (m t) -> p t m", t=PACK),
+        )
+
+        b_sb = []
+        for h in range(2):
+            cols = slice(h * HALF, (h + 1) * HALF)
+            b_ps = ps.tile([P, PACK, HALF], F32, name="b_ps%d" % h)
+            for t in range(PACK):
+                nc.tensor.matmul_mx(
+                    out=b_ps[:, t, :],
+                    lhsT=w2p[:, 2 * P * t : 2 * P * (t + 1)].bitcast(E2M1),
+                    lhsT_scale=wp_s[:, R + P * t : R + P * (t + 1)],
+                    rhs=xg_w[:, cols].bitcast(E4M3),
+                    rhs_scale=xg_s[:, cols],
+                    start=True,
+                    stop=True,
+                )
+            b_h = tile("b_sb%d" % h, [P, HALF, PACK], F32)
+            nc.scalar.copy(b_h[:], b_ps[:].rearrange("p t j -> p j t"))
+            b_sb.append(b_h)
+
+        g = tile("g", [P, PACK, J], BF16)
+        for t in range(PACK):
+            nc.scalar.activation(g[:, t, :], cq_sb[t][:].indirect(l1[:]), COPY, scale=ga_sb[:, t : t + 1])
+
+        wp = tile("wp", [P, R], U32)
+        nc.scalar.copy(
+            wp[:].rearrange("p (t m) -> p t m", t=PACK),
+            w_w[:].bitcast(U32).rearrange("p (m t) -> p t m", t=PACK),
+        )
+
+        x1 = [tile("x1_%d" % h, [P, HALF * PACK], BF16) for h in range(2)]
+        for h in range(2):
+            nc.vector.tensor_copy(
+                x1[h][:].rearrange("p (c i t) -> p c t i", i=4, t=PACK),
+                g[:, :, h * HALF : (h + 1) * HALF].rearrange("p t (c i) -> p c t i", i=4),
+            )
+        xq_w = [tile("xq_w%d" % h, [P, HALF], U32) for h in range(2)]
+        xq_s = [tile("xq_s%d" % h, [P, HALF], U8) for h in range(2)]
+        for h in range(2):
+            nc.vector.quantize_mx(out=xq_w[h][:].bitcast(E4M3), scales=xq_s[h][:], in_=x1[h][:])
+
+        hid = []
+        for h in range(2):
+            a_ps = ps.tile([P, PACK, HALF], F32, name="a_ps%d" % h)
+            for t in range(PACK):
+                nc.tensor.matmul_mx(
+                    out=a_ps[:, t, :],
+                    lhsT=wp[:, P * t : P * (t + 1)].bitcast(E4M3),
+                    lhsT_scale=wp_s[:, P * t : P * (t + 1)],
+                    rhs=xq_w[h][:].bitcast(E4M3),
+                    rhs_scale=xq_s[h][:],
+                    start=True,
+                    stop=True,
+                )
+            hid_h = tile("hid%d" % h, [P, HALF * PACK], BF16)
+            nc.vector.tensor_tensor(
+                hid_h[:].rearrange("p (j t) -> p j t", t=PACK),
+                a_ps[:].rearrange("p t j -> p j t"),
+                b_sb[h][:],
+                MAX,
+            )
+            hid.append(hid_h)
+
+        p_sb = [tile("p_sb%d" % m, [P, J], F32) for m in range(2)]
+        for h in range(2):
+            cols = slice(h * HALF, (h + 1) * HALF)
+            hq_w = tile("hq_w%d" % h, [P, HALF], U32)
+            hq_s = tile("hq_s%d" % h, [P, HALF], U8)
+            nc.vector.quantize_mx(out=hq_w[:].bitcast(E5M2), scales=hq_s[:], in_=hid[h][:])
+            for m in range(2):
+                p_ps = ps.tile([P, HALF], F32, name="p_ps%d%d" % (h, m))
+                nc.tensor.matmul_mx(
+                    out=p_ps[:],
+                    lhsT=wb_w[:, 2 * P * m : 2 * P * (m + 1)].bitcast(E2M1),
+                    lhsT_scale=ws[:, 2 * R + P * m : 2 * R + P * (m + 1)],
+                    rhs=hq_w[:].bitcast(E5M2),
+                    rhs_scale=hq_s[:],
+                    start=True,
+                    stop=True,
+                )
+                if h == 1 and m == 1:
+                    nc.vector.tensor_copy(p_sb[m][:, cols], p_ps[:])
+                else:
+                    nc.scalar.copy(p_sb[m][:, cols], p_ps[:])
+
+        for m in range(2):
+            second = tile("second%d" % m, [P, U], F32)
+            nc.scalar.activation(second[:], p_sb[m][:].indirect(l4[:]), COPY, scale=so_sb[:, m : m + 1])
+            first = tile("first%d" % m, [P, U], F32)
+            nc.vector.tensor_copy(first[:], p_sb[m][:].indirect(l3[:]))
+            y = tile("y%d" % m, [P, U], F32)
+            nc.vector.tensor_tensor(y[:], first[:], second[:], SUB)
+            (nc.scalar if m == 0 else nc.sync).dma_start(out[m * P : (m + 1) * P, :], y[:])

@@ -58,24 +58,25 @@ def tile_list_meetdirect_codednote_one_weighedout_kernel(
 
         cq_rows = cq.rearrange("(p t) c -> p t c", t=PACK)
 
-        nc.sync.dma_start(l1[:], offs)
         nc.scalar.dma_start(ga_sb[:], ga.rearrange("(p t) o -> p (t o)", t=PACK))
-        nc.sync.dma_start(l2[:], offs2)
-        nc.scalar.dma_start(xs_stage[:], rows(xo_scales))
         nc.sync.dma_start(xo_w[:], xo_words[0].rearrange("p n t -> p (n t)").bitcast(I32))
-        nc.scalar.dma_start(ws_stage[:, :, R // 4 : R // 2], rows(w2_scales))
-        nc.sync.dma_start(cq_sb[0][:], cq_rows[:, 0, :])
+        nc.scalar.dma_start(xs_stage[:], rows(xo_scales))
+        nc.sync.dma_start(l2[:], offs2)
         nc.scalar.dma_start(ws_stage[:, :, 0 : R // 4], rows(w_scales))
-        nc.gpsimd.dma_start(ws_stage[:, :, R // 2 : WS], rows(wb_scales))
-        with nc.allow_non_contiguous_dma(reason="one value a partition"):
-            nc.gpsimd.dma_start(so_sb[:], so.rearrange("(m p) o -> p (m o)", p=P))
-        nc.sync.dma_start(w2_w[:], w2_words[0].bitcast(I32))
-        for t in range(1, PACK):
+        nc.sync.dma_start(cq_sb[0][:], cq_rows[:, 0, :])
+        nc.sync.dma_start(l1[:], offs)
+        nc.sync.dma_start(cq_sb[1][:], cq_rows[:, 1, :])
+        nc.sync.dma_start(ws_stage[:, :, R // 4 : R // 2], rows(w2_scales))
+        nc.sync.dma_start(ws_stage[:, :, R // 2 : WS], rows(wb_scales))
+        for t in range(2, PACK):
             nc.sync.dma_start(cq_sb[t][:], cq_rows[:, t, :])
+        nc.sync.dma_start(w2_w[:], w2_words[0].bitcast(I32))
         nc.sync.dma_start(w_w[:], w_words[0].rearrange("p n t -> p (n t)").bitcast(I32))
         nc.sync.dma_start(wb_w[:].bitcast(I32), wb_words[0].bitcast(I32))
         nc.sync.dma_start(l3[:], offs3)
         nc.sync.dma_start(l4[:], offs4)
+        with nc.allow_non_contiguous_dma(reason="one value a partition"):
+            nc.sync.dma_start(so_sb[:], so.rearrange("(m p) o -> p (m o)", p=P))
 
         nc.vector.memset(xs[:].bitcast(I32), 0)
         nc.vector.memset(ws[:].bitcast(I32), 0)
@@ -98,6 +99,16 @@ def tile_list_meetdirect_codednote_one_weighedout_kernel(
             w2_w[:].bitcast(U16).rearrange("p (m t) -> p t m", t=PACK),
         )
 
+        g = [tile("g%d" % u, [P, 2, J], BF16) for u in range(2)]
+        for t in range(PACK):
+            nc.scalar.activation(g[t // 2][:, t % 2, :], cq_sb[t][:].indirect(l1[:]), COPY, scale=ga_sb[:, t : t + 1])
+
+        wp = tile("wp", [P, R], U32)
+        nc.scalar.copy(
+            wp[:].rearrange("p (t m) -> p t m", t=PACK),
+            w_w[:].bitcast(U32).rearrange("p (m t) -> p t m", t=PACK),
+        )
+
         b_sb = []
         for h in range(2):
             cols = slice(h * HALF, (h + 1) * HALF)
@@ -116,22 +127,13 @@ def tile_list_meetdirect_codednote_one_weighedout_kernel(
             nc.scalar.copy(b_h[:], b_ps[:].rearrange("p t j -> p j t"))
             b_sb.append(b_h)
 
-        g = tile("g", [P, PACK, J], BF16)
-        for t in range(PACK):
-            nc.scalar.activation(g[:, t, :], cq_sb[t][:].indirect(l1[:]), COPY, scale=ga_sb[:, t : t + 1])
-
-        wp = tile("wp", [P, R], U32)
-        nc.scalar.copy(
-            wp[:].rearrange("p (t m) -> p t m", t=PACK),
-            w_w[:].bitcast(U32).rearrange("p (m t) -> p t m", t=PACK),
-        )
-
         x1 = [tile("x1_%d" % h, [P, HALF * PACK], BF16) for h in range(2)]
-        for h in range(2):
-            nc.vector.tensor_copy(
-                x1[h][:].rearrange("p (c i t) -> p c t i", i=4, t=PACK),
-                g[:, :, h * HALF : (h + 1) * HALF].rearrange("p t (c i) -> p c t i", i=4),
-            )
+        for u in range(2):
+            for h in range(2):
+                nc.vector.tensor_copy(
+                    x1[h][:].rearrange("p (c t) -> p c t", t=PACK)[:, :, 2 * u : 2 * u + 2],
+                    g[u][:, :, h * HALF : (h + 1) * HALF].rearrange("p t c -> p c t"),
+                )
         xq_w = [tile("xq_w%d" % h, [P, HALF], U32) for h in range(2)]
         xq_s = [tile("xq_s%d" % h, [P, HALF], U8) for h in range(2)]
         for h in range(2):

from contextlib import ExitStack

import concourse.mybir as mybir

K, T, J, R, F, Z, N, U = 512, 1024, 256, 512, 512, 1024, 256, 128
FLOPS = 2 * K * R * J + 2 * F * R * J + 2 * R * N * J

F32 = mybir.dt.float32
BF16 = mybir.dt.bfloat16
I32 = mybir.dt.int32
U32 = mybir.dt.uint32
U16 = mybir.dt.uint16
U8 = mybir.dt.uint8
E4M3 = mybir.dt.float8_e4m3fn_x4
E5M2 = mybir.dt.float8_e5m2_x4
E2M1 = mybir.dt.float4_e2m1fn_x4
COPY = mybir.ActivationFunctionType.Copy
MAX = mybir.AluOpType.max
SUB = mybir.AluOpType.subtract

P = 128
PACK = 4
QUADS = 4
HALF = J // 2


def tile_list_meetdirect_codednote_one_weighedout_kernel(
    tc, cq, ga, w_words, w_scales, xo_words, xo_scales, w2_words, w2_scales, wb_words, wb_scales, so,
    offs, offs2, offs3, offs4, out,
):
    nc = tc.nc
    with ExitStack() as ctx:
        sb = ctx.enter_context(tc.tile_pool(name="sb", bufs=1))
        ps = ctx.enter_context(tc.psum_pool(name="ps", bufs=1))

        def tile(name, shape, dtype):
            return sb.tile(shape, dtype, name=name, align_bytes=64)

        l1 = tile("l1", [P, J // 16], U16)
        l2 = tile("l2", [P, J // 16], U16)
        l3 = tile("l3", [P, U // 16], U16)
        l4 = tile("l4", [P, U // 16], U16)
        ga_sb = tile("ga_sb", [P, PACK], F32)
        so_sb = tile("so_sb", [P, 2], F32)
        cq_sb = [tile("cq%d" % t, [P, T], F32) for t in range(PACK)]
        xo_w = tile("xo_w", [P, Z], I32)
        w_w = tile("w_w", [P, R], I32)
        w2_w = tile("w2_w", [P, R // 2], I32)
        wb_w = tile("wb_w", [P, 2 * N], U8)
        xs_stage = tile("xs_stage", [PACK, QUADS, Z // 4], I32)
        WS = (R + R + N) // 4
        ws_stage = tile("ws_stage", [PACK, QUADS, WS], I32)
        xs = tile("xs", [P, Z], U8)
        ws = tile("ws", [P, R + R + N], U8)

        def rows(scales):
            return scales[0].bitcast(I32).rearrange("(q r) n -> r q n", r=PACK)

        cq_rows = cq.rearrange("(p t) c -> p t c", t=PACK)

        nc.scalar.dma_start(ga_sb[:], ga.rearrange("(p t) o -> p (t o)", t=PACK))
        nc.sync.dma_start(xo_w[:], xo_words[0].rearrange("p n t -> p (n t)").bitcast(I32))
        nc.scalar.dma_start(xs_stage[:], rows(xo_scales))
        nc.sync.dma_start(l2[:], offs2)
        nc.scalar.dma_start(ws_stage[:, :, 0 : R // 4], rows(w_scales))
        nc.sync.dma_start(cq_sb[0][:], cq_rows[:, 0, :])
        nc.sync.dma_start(l1[:], offs)
        nc.sync.dma_start(cq_sb[1][:], cq_rows[:, 1, :])
        nc.sync.dma_start(ws_stage[:, :, R // 4 : R // 2], rows(w2_scales))
        nc.sync.dma_start(ws_stage[:, :, R // 2 : WS], rows(wb_scales))
        for t in range(2, PACK):
            nc.sync.dma_start(cq_sb[t][:], cq_rows[:, t, :])
        nc.sync.dma_start(w2_w[:], w2_words[0].bitcast(I32))
        nc.sync.dma_start(w_w[:], w_words[0].rearrange("p n t -> p (n t)").bitcast(I32))
        nc.sync.dma_start(wb_w[:].bitcast(I32), wb_words[0].bitcast(I32))
        nc.sync.dma_start(l3[:], offs3)
        nc.sync.dma_start(l4[:], offs4)
        with nc.allow_non_contiguous_dma(reason="one value a partition"):
            nc.sync.dma_start(so_sb[:], so.rearrange("(m p) o -> p (m o)", p=P))

        nc.vector.memset(xs[:].bitcast(I32), 0)
        nc.vector.memset(ws[:].bitcast(I32), 0)
        for q in range(QUADS):
            nc.vector.tensor_copy(xs[32 * q : 32 * q + PACK, :].bitcast(I32), xs_stage[:, q, :])
        xg_s = tile("xg_s", [P, J], U8)
        nc.vector.tensor_copy(xg_s[:], xs[:].indirect(l2[:]))
        xg_w = tile("xg_w", [P, J], U32)
        nc.vector.tensor_copy(xg_w[:], xo_w[:].bitcast(U32).indirect(l2[:]))
        for q in range(QUADS):
            nc.vector.tensor_copy(ws[32 * q : 32 * q + PACK, :].bitcast(I32), ws_stage[:, q, :])
        wp_s = tile("wp_s", [P, 2 * R], U8)
        nc.vector.tensor_copy(
            wp_s[:].rearrange("p (g t m) -> p g t m", g=2, t=PACK),
            ws[:, 0 : 2 * R].rearrange("p (g m t) -> p g t m", g=2, t=PACK),
        )
        w2p = tile("w2p", [P, 2 * R], U8)
        nc.vector.tensor_copy(
            w2p[:].bitcast(U16).rearrange("p (t m) -> p t m", t=PACK),
            w2_w[:].bitcast(U16).rearrange("p (m t) -> p t m", t=PACK),
        )

        g = [tile("g%d" % u, [P, 2, J], BF16) for u in range(2)]
        for t in range(PACK):
            nc.scalar.activation(g[t // 2][:, t % 2, :], cq_sb[t][:].indirect(l1[:]), COPY, scale=ga_sb[:, t : t + 1])

        wp = tile("wp", [P, R], U32)
        nc.scalar.copy(
            wp[:].rearrange("p (t m) -> p t m", t=PACK),
            w_w[:].bitcast(U32).rearrange("p (m t) -> p t m", t=PACK),
        )

        b_sb = []
        for h in range(2):
            cols = slice(h * HALF, (h + 1) * HALF)
            b_ps = ps.tile([P, PACK, HALF], F32, name="b_ps%d" % h)
            for t in range(PACK):
                nc.tensor.matmul_mx(
                    out=b_ps[:, t, :],
                    lhsT=w2p[:, 2 * P * t : 2 * P * (t + 1)].bitcast(E2M1),
                    lhsT_scale=wp_s[:, R + P * t : R + P * (t + 1)],
                    rhs=xg_w[:, cols].bitcast(E4M3),
                    rhs_scale=xg_s[:, cols],
                    start=True,
                    stop=True,
                )
            b_h = tile("b_sb%d" % h, [P, HALF, PACK], F32)
            nc.scalar.copy(b_h[:], b_ps[:].rearrange("p t j -> p j t"))
            b_sb.append(b_h)

        x1 = [tile("x1_%d" % h, [P, HALF * PACK], BF16) for h in range(2)]
        for u in range(2):
            for h in range(2):
                nc.vector.tensor_copy(
                    x1[h][:].rearrange("p (c t) -> p c t", t=PACK)[:, :, 2 * u : 2 * u + 2],
                    g[u][:, :, h * HALF : (h + 1) * HALF].rearrange("p t c -> p c t"),
                )
        xq_w = [tile("xq_w%d" % h, [P, HALF], U32) for h in range(2)]
        xq_s = [tile("xq_s%d" % h, [P, HALF], U8) for h in range(2)]
        for h in range(2):
            nc.vector.quantize_mx(out=xq_w[h][:].bitcast(E4M3), scales=xq_s[h][:], in_=x1[h][:])

        hid = []
        for h in range(2):
            a_ps = ps.tile([P, PACK, HALF], F32, name="a_ps%d" % h)
            for t in range(PACK):
                nc.tensor.matmul_mx(
                    out=a_ps[:, t, :],
                    lhsT=wp[:, P * t : P * (t + 1)].bitcast(E4M3),
                    lhsT_scale=wp_s[:, P * t : P * (t + 1)],
                    rhs=xq_w[h][:].bitcast(E4M3),
                    rhs_scale=xq_s[h][:],
                    start=True,
                    stop=True,
                )
            hid_h = tile("hid%d" % h, [P, HALF * PACK], BF16)
            nc.vector.tensor_tensor(
                hid_h[:].rearrange("p (j t) -> p j t", t=PACK),
                a_ps[:].rearrange("p t j -> p j t"),
                b_sb[h][:],
                MAX,
            )
            hid.append(hid_h)

        p_sb = [tile("p_sb%d" % m, [P, J], F32) for m in range(2)]
        for h in range(2):
            cols = slice(h * HALF, (h + 1) * HALF)
            hq_w = tile("hq_w%d" % h, [P, HALF], U32)
            hq_s = tile("hq_s%d" % h, [P, HALF], U8)
            nc.vector.quantize_mx(out=hq_w[:].bitcast(E5M2), scales=hq_s[:], in_=hid[h][:])
            for m in range(2):
                p_ps = ps.tile([P, HALF], F32, name="p_ps%d%d" % (h, m))
                nc.tensor.matmul_mx(
                    out=p_ps[:],
                    lhsT=wb_w[:, 2 * P * m : 2 * P * (m + 1)].bitcast(E2M1),
                    lhsT_scale=ws[:, 2 * R + P * m : 2 * R + P * (m + 1)],
                    rhs=hq_w[:].bitcast(E5M2),
                    rhs_scale=hq_s[:],
                    start=True,
                    stop=True,
                )
                if h == 1 and m == 1:
                    nc.vector.tensor_copy(p_sb[m][:, cols], p_ps[:])
                else:
                    nc.scalar.copy(p_sb[m][:, cols], p_ps[:])

        for m in range(2):
            second = tile("second%d" % m, [P, U], F32)
            nc.scalar.activation(second[:], p_sb[m][:].indirect(l4[:]), COPY, scale=so_sb[:, m : m + 1])
            first = tile("first%d" % m, [P, U], F32)
            nc.vector.tensor_copy(first[:], p_sb[m][:].indirect(l3[:]))
            y = tile("y%d" % m, [P, U], F32)
            nc.vector.tensor_tensor(y[:], first[:], second[:], SUB)
            (nc.scalar if m == 0 else nc.sync).dma_start(out[m * P : (m + 1) * P, :], y[:])
